import numpy as np
import ml_dtypes


def mxq(x, axis, fmt="e4m3"):
    dtype, down = {"e4m3": (ml_dtypes.float8_e4m3fn, 7), "e5m2": (ml_dtypes.float8_e5m2, 14)}[fmt]
    v = np.moveaxis(np.asarray(x, np.float32).astype(ml_dtypes.bfloat16).astype(np.float64), axis, -1)
    blocks = v.reshape(v.shape[:-1] + (-1, 32))
    amax = np.abs(blocks).max(-1, keepdims=True)
    byte = np.maximum(np.where(amax > 0, np.frexp(amax)[1] - 1 + 127, 0) - down, 1)
    scale = np.exp2(byte - 127.0)
    codes = (blocks / scale).astype(np.float32).astype(dtype).astype(np.float64)
    return np.moveaxis((codes * scale).reshape(v.shape), -1, axis)


WIDE = False


def mx_kscale(k):
    if not WIDE:
        return np.ones(k)
    levels = np.array([10, -10, 5, -5, 0])
    if k % 512:
        return np.exp2(np.random.permutation(np.resize(levels, k // 32))).repeat(32)
    a = np.empty((k // 512, 16))
    for p in range(k // 512):
        a[p, :8] = np.random.permutation(np.resize(levels, 8))
        for g in range(8):
            far = levels[np.abs(levels - a[p, g]) >= 10]
            a[p, g + 8] = far[np.random.randint(len(far))]
    return np.exp2(a.ravel()).repeat(32)


def f64(x):
    return np.asarray(x).astype(np.float64)


def striped(idx):
    return np.tile(idx.reshape(-1, 16).T, (8, 1)).astype(np.uint16)


def unstriped(offs):
    return offs[:16].T.reshape(-1).astype(np.int64)


def striped8(idx):
    return np.concatenate([x.reshape(-1, 16).T for x in idx]).astype(np.uint16)


def runs(offs, k):
    lists = np.stack([offs[16 * r : 16 * r + 16].T.reshape(-1) for r in range(8)]).astype(np.int64)
    return lists[np.arange(k) % 512 // 64]


def pack_weight(w):
    k, n = w.shape
    w = f64(np.asarray(w, np.float32).astype(ml_dtypes.bfloat16)).reshape(k // 32, 32, n)
    amax = np.abs(w).max(1)
    byte = np.clip(np.where(amax > 0, np.frexp(amax)[1] - 1 + 127 - 7, 1), 1, 254)
    scaled = (w * np.exp2(127.0 - byte)[:, None, :]).reshape(k, n).astype(np.float32)
    words = np.ascontiguousarray(scaled.reshape(k // 512, 128, 4, n).transpose(0, 1, 3, 2)).astype(ml_dtypes.float8_e4m3fn).view(np.uint8)
    return words, np.ascontiguousarray(byte.astype(np.uint8).reshape(k // 512, 16, n))


def unpack_weight(words, scales):
    g, p, n, _ = words.shape
    vals = np.ascontiguousarray(words).view(ml_dtypes.float8_e4m3fn).astype(np.float64) * np.repeat(np.exp2(scales.astype(np.float64) - 127.0), 8, axis=1)[..., None]
    return vals.transpose(0, 1, 3, 2).reshape(g * 512, n)


K, T, S, G, H, W = 512, 1024, 512, 2048, 512, 256


def setup_inputs():
    n = np.random.standard_normal
    s = mx_kscale(K)[:, None]
    packed_xT = pack_weight(n((K, T)) * s)
    packed_dT = pack_weight(n((K, G)) / s)
    perm = np.stack([np.random.permutation(S) for _ in range(8)])
    return {
        "x_words": packed_xT[0],
        "x_scales": packed_xT[1],
        "d_words": packed_dT[0],
        "d_scales": packed_dT[1],
        "gs": (np.random.uniform(0.5, 1.5, (K, 1)) * s).astype(np.float32),
        "offs": striped(np.random.permutation(T)[:S]),
        "k1": striped8(np.random.randint(0, G, (8, H))),
        "n1": striped8(np.stack([np.random.permutation(S) for _ in range(8)])),
        "n2": striped8(np.stack([np.random.permutation(S) for _ in range(8)])),
        "k2": striped8(np.random.randint(0, G, (8, H))),
        "n3": striped8(perm[:, :W]),
        "n4": striped8(perm[:, W:]),
    }


def reference(x_words, x_scales, d_words, d_scales, gs, offs, k1, n1, n2, k2, n3, n4):
    d_k2 = unpack_weight(d_words, d_scales)[np.arange(K)[:, None], runs(k2, K)]
    d_k1 = unpack_weight(d_words, d_scales)[np.arange(K)[:, None], runs(k1, K)]
    xq = unpack_weight(x_words, x_scales)[:, unstriped(offs)]
    h = 0.0625 * (d_k1.T @ xq)
    z = f64(gs) * (h * (h[np.arange(H)[:, None], runs(n1, H)] - (h[np.arange(H)[:, None], runs(n2, H)])))
    h2 = 0.0625 * ((d_k2.T @ mxq(z, 0, "e4m3")))
    pa = h2[np.arange(H)[:, None], runs(n3, H)]
    pb = h2[np.arange(H)[:, None], runs(n4, H)]
    rb = np.minimum(pa, pb)
    ra = np.maximum(pa, pb)
    ds = np.zeros((H, S))
    ds[np.arange(H)[:, None], runs(n3, H)] = ra
    out = ds.copy()
    out[np.arange(H)[:, None], runs(n4, H)] = rb
    return out

@@ -1,0 +1,206 @@
+from contextlib import ExitStack
+
+import concourse.mybir as mybir
+
+K, T, S, G, H, W = 512, 1024, 512, 2048, 512, 256
+FLOPS = 2 * K * H * S * 2
+
+F32 = mybir.dt.float32
+BF16 = mybir.dt.bfloat16
+I32 = mybir.dt.int32
+U32 = mybir.dt.uint32
+U16 = mybir.dt.uint16
+U8 = mybir.dt.uint8
+FP8X4 = mybir.dt.float8_e4m3fn_x4
+ALU = mybir.AluOpType
+ACT = mybir.ActivationFunctionType
+
+P = 128
+PACK = 4
+HALF = S // 2
+
+
+def tile_picked_codewindorder_none_p_kernel(
+    tc, x_words, x_scales, d_words, d_scales, gs, offs, k1, n1, n2, k2, n3, n4, out
+):
+    nc = tc.nc
+    with ExitStack() as ctx:
+        keep = ctx.enter_context(tc.tile_pool(name="keep", bufs=1))
+        psum = ctx.enter_context(tc.psum_pool(name="psum", bufs=1))
+
+        def sb(name, cols, dtype):
+            return keep.tile([P, cols], dtype, name=name, align_bytes=64)
+
+        def load_list(name, src):
+            t = sb(name, src.shape[1], U16)
+            nc.sync.dma_start(t[:], src)
+            return t
+
+        d_bytes = sb("d_bytes", G, U8)
+        x_bytes = sb("x_bytes", T, U8)
+        nc.vector.memset(d_bytes[:].bitcast(I32), 0)
+        nc.vector.memset(x_bytes[:].bitcast(I32), 0)
+
+        k1_l = load_list("k1_l", k1)
+        d_rows = d_scales[0].rearrange("(r a) c -> a r c", a=2)
+        for a in range(2):
+            nc.sync.dma_start(d_bytes[a:P:16, :].bitcast(I32), d_rows[a].bitcast(I32))
+        offs_l = load_list("offs_l", offs)
+        for q in range(4):
+            nc.scalar.dma_start(
+                x_bytes[32 * q : 32 * q + 4, :].bitcast(I32),
+                x_scales[0, 4 * q : 4 * q + 4, :].bitcast(I32),
+            )
+        x_tab = sb("x_tab", T, U32)
+        nc.sync.dma_start(x_tab[:].bitcast(I32), x_words[0].rearrange("p n t -> p (n t)").bitcast(I32))
+        d_tab = sb("d_tab", G, U32)
+        nc.sync.dma_start(d_tab[:].bitcast(I32), d_words[0].rearrange("p n t -> p (n t)").bitcast(I32))
+        k2_l = load_list("k2_l", k2)
+        n2_l = load_list("n2_l", n2)
+        n1_l = load_list("n1_l", n1)
+        n4_l = load_list("n4_l", n4)
+        n3_l = load_list("n3_l", n3)
+        gs_raw = sb("gs_raw", PACK, F32)
+        nc.scalar.dma_start(gs_raw[:], gs.rearrange("(p t) o -> p (t o)", t=PACK))
+        gain = sb("gain", PACK, F32)
+        nc.scalar.activation(gain[:], gs_raw[:], ACT.Copy, scale=0.0625 * 0.0625)
+
+        hw = [sb("hw%d" % t, 2 * S, F32) for t in range(PACK)]
+        for t in range(PACK):
+            nc.vector.memset(hw[t][:, S:], 0.0)
+
+        def pick_scales(name, lst):
+            got = sb(name + "_got", H, U8)
+            nc.vector.tensor_copy(got[:], d_bytes[:].indirect(lst[:]))
+            dealt = sb(name + "_dealt", H, U8)
+            nc.vector.tensor_copy(
+                dealt[:].rearrange("p (t c i) -> p c t i", t=PACK, i=16),
+                got[:].rearrange("p (c i t) -> p c t i", t=PACK, i=16),
+            )
+            for a in range(2):
+                nc.sync.dma_start(dealt[2 + a : P : 32, :].bitcast(I32), dealt[16 + a : P : 32, :].bitcast(I32))
+            return dealt
+
+        def gather_words(name, lst):
+            got = sb(name + "_got", H, U32)
+            nc.vector.tensor_copy(got[:], d_tab[:].indirect(lst[:]))
+            return got
+
+        def deal_words(name, got):
+            dealt = sb(name + "_dealt", H, U32)
+            nc.vector.tensor_copy(
+                dealt[:].rearrange("p (t c i) -> p c t i", t=PACK, i=4),
+                got[:].rearrange("p (c i t) -> p c t i", t=PACK, i=4),
+            )
+            return dealt
+
+        w1_s = pick_scales("w1s", k1_l)
+        xq_s = sb("xq_s", S, U8)
+        nc.vector.tensor_copy(xq_s[:], x_bytes[:].indirect(offs_l[:]))
+        xq_w = sb("xq_w", S, U32)
+        nc.vector.tensor_copy(xq_w[:], x_tab[:].indirect(offs_l[:]))
+        w1_w = deal_words("w1w", gather_words("w1w", k1_l))
+
+        banks = [psum.tile([P, S], F32, name="bank%d" % b) for b in range(8)]
+        for t in range(PACK):
+            cols = slice(t * P, (t + 1) * P)
+            nc.tensor.matmul_mx(
+                out=banks[t][:],
+                lhsT=w1_w[:, cols].bitcast(FP8X4),
+                lhsT_scale=w1_s[:, cols],
+                rhs=xq_w[:].bitcast(FP8X4),
+                rhs_scale=xq_s[:],
+                start=True,
+                stop=True,
+            )
+            nc.scalar.copy(hw[t][:, :S], banks[t][:])
+
+        w2_s = pick_scales("w2s", k2_l)
+
+        second = [sb("second%d" % t, S, F32) for t in range(PACK)]
+        diff = [sb("diff%d" % t, S, F32) for t in range(PACK)]
+        z_rows = [sb("z_rows%d" % u, PACK * HALF, BF16) for u in range(2)]
+        z_mix = [sb("z_mix%d" % u, PACK * HALF, BF16) for u in range(2)]
+        z_w = [sb("z_w%d" % u, HALF, U32) for u in range(2)]
+        z_s = [sb("z_s%d" % u, HALF, U8) for u in range(2)]
+
+        def gathers(ts, lo, hi):
+            lc = slice(lo // 16, hi // 16)
+            for t in ts:
+                nc.vector.tensor_copy(second[t][:, lo:hi], hw[t][:].indirect(n2_l[:, lc]))
+            for t in ts:
+                nc.vector.tensor_tensor(
+                    diff[t][:, lo:hi], hw[t][:].indirect(n1_l[:, lc]), second[t][:, lo:hi], ALU.subtract
+                )
+
+        def products(ts, u):
+            c = slice(u * HALF, (u + 1) * HALF)
+            for t in ts:
+                nc.vector.scalar_tensor_tensor(
+                    z_rows[u][:, t * HALF : (t + 1) * HALF],
+                    diff[t][:, c],
+                    gain[:, t : t + 1],
+                    hw[t][:, c],
+                    ALU.mult,
+                    ALU.mult,
+                )
+
+        def interleave(u):
+            nc.scalar.copy(
+                z_mix[u][:].rearrange("p (c i t) -> p c t i", t=PACK, i=4),
+                z_rows[u][:].rearrange("p (t c i) -> p c t i", t=PACK, i=4),
+            )
+
+        def quantize(u):
+            nc.vector.quantize_mx(out=z_w[u][:].bitcast(FP8X4), scales=z_s[u][:], in_=z_mix[u][:])
+
+        gathers((0, 1), 0, S)
+        products((0, 1), 0)
+        products((0, 1), 1)
+        gathers((2, 3), 0, HALF)
+        products((2, 3), 0)
+        interleave(0)
+        gathers((2, 3), HALF, S)
+        products((2, 3), 1)
+        interleave(1)
+        quantize(0)
+        w2_w = deal_words("w2w", gather_words("w2w", k2_l))
+        quantize(1)
+
+        h2 = [sb("h2_%d" % t, S, F32) for t in range(PACK)]
+        for t in range(PACK):
+            cols = slice(t * P, (t + 1) * P)
+            for u in range(2):
+                acc = banks[4 * (1 - u) + t]
+                nc.tensor.matmul_mx(
+                    out=acc[:, :HALF],
+                    lhsT=w2_w[:, cols].bitcast(FP8X4),
+                    lhsT_scale=w2_s[:, cols],
+                    rhs=z_w[u][:].bitcast(FP8X4),
+                    rhs_scale=z_s[u][:],
+                    start=True,
+                    stop=True,
+                )
+                nc.scalar.activation(h2[t][:, u * HALF : (u + 1) * HALF], acc[:, :HALF], ACT.Copy, scale=0.0625)
+
+        pb = [sb("pb%d" % t, W, F32) for t in range(PACK)]
+        gap = [sb("gap%d" % t, W, F32) for t in range(PACK)]
+        up = [sb("up%d" % t, W, F32) for t in range(PACK)]
+        drop = [sb("drop%d" % t, W, F32) for t in range(PACK)]
+        down = [sb("down%d" % t, W, F32) for t in range(PACK)]
+        res = [sb("res%d" % t, S, F32) for t in range(PACK)]
+        out_rows = out.rearrange("(p t) n -> t p n", t=PACK)
+        for ts in ((0, 1), (2, 3)):
+            for t in ts:
+                nc.vector.tensor_copy(pb[t][:], h2[t][:].indirect(n4_l[:]))
+            for t in ts:
+                nc.vector.tensor_tensor(gap[t][:], h2[t][:].indirect(n3_l[:]), pb[t][:], ALU.subtract)
+                nc.scalar.activation(up[t][:], gap[t][:], ACT.Relu)
+                nc.scalar.activation(drop[t][:], gap[t][:], ACT.Relu, scale=-1.0)
+                nc.scalar.activation(down[t][:], drop[t][:], ACT.Copy, scale=-1.0)
+        for ts in ((0, 1), (2, 3)):
+            for t in ts:
+                nc.vector.tensor_tensor(res[t][:].indirect(n3_l[:]), pb[t][:], up[t][:], ALU.add)
+            for t in ts:
+                nc.vector.tensor_tensor(res[t][:].indirect(n4_l[:]), pb[t][:], down[t][:], ALU.add)
+                nc.sync.dma_start(out_rows[t], res[t][:])

@@ -36,21 +36,17 @@ def tile_picked_codewindorder_none_p_kernel(
             nc.sync.dma_start(t[:], src)
             return t
 
-        d_bytes = sb("d_bytes", G, U8)
-        x_bytes = sb("x_bytes", T, U8)
-        nc.vector.memset(d_bytes[:].bitcast(I32), 0)
-        nc.vector.memset(x_bytes[:].bitcast(I32), 0)
+        def load_scale_rows(name, src):
+            cols = src.shape[2]
+            t = sb(name, cols, U8)
+            rows = src[0].bitcast(I32)
+            nc.sync.dma_start(t[:].bitcast(I32), rows.unsqueeze(1).to_broadcast([16, 8, cols // 4]))
+            return t
 
-        k1_l = load_list("k1_l", k1)
-        d_rows = d_scales[0].rearrange("(r a) c -> a r c", a=2)
-        for a in range(2):
-            nc.sync.dma_start(d_bytes[a:P:16, :].bitcast(I32), d_rows[a].bitcast(I32))
         offs_l = load_list("offs_l", offs)
-        for q in range(4):
-            nc.scalar.dma_start(
-                x_bytes[32 * q : 32 * q + 4, :].bitcast(I32),
-                x_scales[0, 4 * q : 4 * q + 4, :].bitcast(I32),
-            )
+        x_bytes = load_scale_rows("x_bytes", x_scales)
+        k1_l = load_list("k1_l", k1)
+        d_bytes = load_scale_rows("d_bytes", d_scales)
         x_tab = sb("x_tab", T, U32)
         nc.sync.dma_start(x_tab[:].bitcast(I32), x_words[0].rearrange("p n t -> p (n t)").bitcast(I32))
         d_tab = sb("d_tab", G, U32)
@@ -67,19 +63,19 @@ def tile_picked_codewindorder_none_p_kernel(
 
         hw = [sb("hw%d" % t, 2 * S, F32) for t in range(PACK)]
         for t in range(PACK):
-            nc.vector.memset(hw[t][:, S:], 0.0)
+            (nc.vector if t < 2 else nc.gpsimd).memset(hw[t][:, S:], 0.0)
 
-        def pick_scales(name, lst):
+        def pick_scales(name, lst, dealt):
             got = sb(name + "_got", H, U8)
             nc.vector.tensor_copy(got[:], d_bytes[:].indirect(lst[:]))
-            dealt = sb(name + "_dealt", H, U8)
             nc.vector.tensor_copy(
-                dealt[:].rearrange("p (t c i) -> p c t i", t=PACK, i=16),
+                dealt.rearrange("p (t c i) -> p c t i", t=PACK, i=16),
                 got[:].rearrange("p (c i t) -> p c t i", t=PACK, i=16),
             )
-            for a in range(2):
-                nc.sync.dma_start(dealt[2 + a : P : 32, :].bitcast(I32), dealt[16 + a : P : 32, :].bitcast(I32))
-            return dealt
+
+        def compact_rows(plane):
+            for a in range(1, 4):
+                nc.sync.dma_start(plane[a:P:32, :].bitcast(I32), plane[8 * a : P : 32, :].bitcast(I32))
 
         def gather_words(name, lst):
             got = sb(name + "_got", H, U32)
@@ -94,9 +90,17 @@ def tile_picked_codewindorder_none_p_kernel(
             )
             return dealt
 
-        w1_s = pick_scales("w1s", k1_l)
-        xq_s = sb("xq_s", S, U8)
-        nc.vector.tensor_copy(xq_s[:], x_bytes[:].indirect(offs_l[:]))
+        plane1 = sb("plane1", H + S, U8)
+        xs_got = sb("xs_got", S, U8)
+        nc.vector.tensor_copy(xs_got[:], x_bytes[:].indirect(offs_l[:]))
+        w1s_got = sb("w1s_got", H, U8)
+        nc.vector.tensor_copy(w1s_got[:], d_bytes[:].indirect(k1_l[:]))
+        nc.vector.tensor_copy(plane1[:, H:].bitcast(I32), xs_got[:].bitcast(I32))
+        nc.vector.tensor_copy(
+            plane1[:, :H].rearrange("p (t c i) -> p c t i", t=PACK, i=16),
+            w1s_got[:].rearrange("p (c i t) -> p c t i", t=PACK, i=16),
+        )
+        compact_rows(plane1)
         xq_w = sb("xq_w", S, U32)
         nc.vector.tensor_copy(xq_w[:], x_tab[:].indirect(offs_l[:]))
         w1_w = deal_words("w1w", gather_words("w1w", k1_l))
@@ -107,65 +111,60 @@ def tile_picked_codewindorder_none_p_kernel(
             nc.tensor.matmul_mx(
                 out=banks[t][:],
                 lhsT=w1_w[:, cols].bitcast(FP8X4),
-                lhsT_scale=w1_s[:, cols],
+                lhsT_scale=plane1[:, cols],
                 rhs=xq_w[:].bitcast(FP8X4),
-                rhs_scale=xq_s[:],
+                rhs_scale=plane1[:, H:],
                 start=True,
                 stop=True,
             )
             nc.scalar.copy(hw[t][:, :S], banks[t][:])
 
-        w2_s = pick_scales("w2s", k2_l)
+        w2_s = sb("plane2", H, U8)
+        pick_scales("w2s", k2_l, w2_s[:])
+        compact_rows(w2_s)
 
+        hg = sb("hg", PACK * S, F32)
+        for t in range(PACK):
+            nc.scalar.activation(hg[:, t * S : (t + 1) * S], banks[t][:], ACT.Copy, scale=gain[:, t : t + 1])
         second = [sb("second%d" % t, S, F32) for t in range(PACK)]
-        diff = [sb("diff%d" % t, S, F32) for t in range(PACK)]
-        z_rows = [sb("z_rows%d" % u, PACK * HALF, BF16) for u in range(2)]
-        z_mix = [sb("z_mix%d" % u, PACK * HALF, BF16) for u in range(2)]
+        diff = sb("diff", PACK * S, F32)
+        z_mix = [
+            keep.tile([P, PACK * HALF], BF16, name="z_mix%d" % u, tag="z_mix%d" % u, align_bytes=64) for u in range(2)
+        ]
         z_w = [sb("z_w%d" % u, HALF, U32) for u in range(2)]
         z_s = [sb("z_s%d" % u, HALF, U8) for u in range(2)]
 
-        def gathers(ts, lo, hi):
-            lc = slice(lo // 16, hi // 16)
+        for ts in ((0, 1), (2, 3)):
             for t in ts:
-                nc.vector.tensor_copy(second[t][:, lo:hi], hw[t][:].indirect(n2_l[:, lc]))
+                nc.vector.tensor_copy(second[t][:], hw[t][:].indirect(n2_l[:]))
             for t in ts:
                 nc.vector.tensor_tensor(
-                    diff[t][:, lo:hi], hw[t][:].indirect(n1_l[:, lc]), second[t][:, lo:hi], ALU.subtract
+                    diff[:, t * S : (t + 1) * S], hw[t][:].indirect(n1_l[:]), second[t][:], ALU.subtract
                 )
 
-        def products(ts, u):
-            c = slice(u * HALF, (u + 1) * HALF)
-            for t in ts:
-                nc.vector.scalar_tensor_tensor(
-                    z_rows[u][:, t * HALF : (t + 1) * HALF],
-                    diff[t][:, c],
-                    gain[:, t : t + 1],
-                    hw[t][:, c],
-                    ALU.mult,
-                    ALU.mult,
-                )
-
-        def interleave(u):
-            nc.scalar.copy(
-                z_mix[u][:].rearrange("p (c i t) -> p c t i", t=PACK, i=4),
-                z_rows[u][:].rearrange("p (t c i) -> p c t i", t=PACK, i=4),
+        def product(u):
+            pairs = slice(u * HALF // 2, (u + 1) * HALF // 2)
+            nc.vector.tensor_tensor(
+                z_mix[u][:].rearrange("p (c i t) -> p c t i", t=PACK, i=2),
+                diff[:].rearrange("p (t c i) -> p c t i", t=PACK, i=2)[:, pairs],
+                hg[:].rearrange("p (t c i) -> p c t i", t=PACK, i=2)[:, pairs],
+                ALU.mult,
             )
 
         def quantize(u):
             nc.vector.quantize_mx(out=z_w[u][:].bitcast(FP8X4), scales=z_s[u][:], in_=z_mix[u][:])
 
-        gathers((0, 1), 0, S)
-        products((0, 1), 0)
-        products((0, 1), 1)
-        gathers((2, 3), 0, HALF)
-        products((2, 3), 0)
-        interleave(0)
-        gathers((2, 3), HALF, S)
-        products((2, 3), 1)
-        interleave(1)
+        w2_got = gather_words("w2w", k2_l)
+        product(0)
+        product(1)
+        got4 = w2_got[:].rearrange("p (c i t) -> p c t i", t=PACK, i=4)
         quantize(0)
-        w2_w = deal_words("w2w", gather_words("w2w", k2_l))
+        w2_first = keep.tile([P, P], U32, name="w2_first", tag="z_mix0", align_bytes=64)
+        nc.vector.tensor_copy(w2_first[:].rearrange("p (c i) -> p c i", i=4), got4[:, :, 0, :])
         quantize(1)
+        w2_rest = keep.tile([P, 3 * P], U32, name="w2_rest", tag="z_mix1", align_bytes=64)
+        nc.vector.tensor_copy(w2_rest[:].rearrange("p (t c i) -> p c t i", t=PACK - 1, i=4), got4[:, :, 1:, :])
+        w2_w = [w2_first[:]] + [w2_rest[:, (t - 1) * P : t * P] for t in range(1, PACK)]
 
         h2 = [sb("h2_%d" % t, S, F32) for t in range(PACK)]
         for t in range(PACK):
@@ -174,7 +173,7 @@ def tile_picked_codewindorder_none_p_kernel(
                 acc = banks[4 * (1 - u) + t]
                 nc.tensor.matmul_mx(
                     out=acc[:, :HALF],
-                    lhsT=w2_w[:, cols].bitcast(FP8X4),
+                    lhsT=w2_w[t].bitcast(FP8X4),
                     lhsT_scale=w2_s[:, cols],
                     rhs=z_w[u][:].bitcast(FP8X4),
                     rhs_scale=z_s[u][:],

@@ -43,10 +43,12 @@ def tile_picked_codewindorder_none_p_kernel(
             nc.sync.dma_start(t[:].bitcast(I32), rows.unsqueeze(1).to_broadcast([16, 8, cols // 4]))
             return t
 
-        offs_l = load_list("offs_l", offs)
+        d_bytes = sb("d_bytes", G, U8)
+        nc.vector.memset(d_bytes[:].bitcast(I32), 0)
         x_bytes = load_scale_rows("x_bytes", x_scales)
+        offs_l = load_list("offs_l", offs)
         k1_l = load_list("k1_l", k1)
-        d_bytes = load_scale_rows("d_bytes", d_scales)
+        nc.sync.dma_start(d_bytes[0:P:8, :].bitcast(I32), d_scales[0].bitcast(I32))
         x_tab = sb("x_tab", T, U32)
         nc.sync.dma_start(x_tab[:].bitcast(I32), x_words[0].rearrange("p n t -> p (n t)").bitcast(I32))
         d_tab = sb("d_tab", G, U32)
@@ -123,7 +125,7 @@ def tile_picked_codewindorder_none_p_kernel(
         pick_scales("w2s", k2_l, w2_s[:])
         compact_rows(w2_s)
 
-        hg = sb("hg", PACK * S, F32)
+        hg = keep.tile([P, PACK * S], F32, name="hg", tag="hg", align_bytes=64)
         for t in range(PACK):
             nc.scalar.activation(hg[:, t * S : (t + 1) * S], banks[t][:], ACT.Copy, scale=gain[:, t : t + 1])
         second = [sb("second%d" % t, S, F32) for t in range(PACK)]
@@ -159,10 +161,10 @@ def tile_picked_codewindorder_none_p_kernel(
         product(1)
         got4 = w2_got[:].rearrange("p (c i t) -> p c t i", t=PACK, i=4)
         quantize(0)
-        w2_first = keep.tile([P, P], U32, name="w2_first", tag="z_mix0", align_bytes=64)
+        w2_first = keep.tile([P, P], U32, name="w2_first", tag="hg", align_bytes=64)
         nc.vector.tensor_copy(w2_first[:].rearrange("p (c i) -> p c i", i=4), got4[:, :, 0, :])
         quantize(1)
-        w2_rest = keep.tile([P, 3 * P], U32, name="w2_rest", tag="z_mix1", align_bytes=64)
+        w2_rest = keep.tile([P, 3 * P], U32, name="w2_rest", tag="z_mix0", align_bytes=64)
         nc.vector.tensor_copy(w2_rest[:].rearrange("p (t c i) -> p c t i", t=PACK - 1, i=4), got4[:, :, 1:, :])
         w2_w = [w2_first[:]] + [w2_rest[:, (t - 1) * P : t * P] for t in range(1, PACK)]
 

@@ -26,6 +26,7 @@ def tile_picked_codewindorder_none_p_kernel(
     nc = tc.nc
     with ExitStack() as ctx:
         keep = ctx.enter_context(tc.tile_pool(name="keep", bufs=1))
+        reuse = ctx.enter_context(tc.tile_pool(name="reuse", bufs=1))
         psum = ctx.enter_context(tc.psum_pool(name="psum", bufs=1))
 
         def sb(name, cols, dtype):
@@ -38,22 +39,20 @@ def tile_picked_codewindorder_none_p_kernel(
 
         def load_scale_rows(name, src):
             cols = src.shape[2]
-            t = sb(name, cols, U8)
+            t = keep.tile([P, cols], U8, name=name, tag=name, align_bytes=64)
             rows = src[0].bitcast(I32)
             nc.sync.dma_start(t[:].bitcast(I32), rows.unsqueeze(1).to_broadcast([16, 8, cols // 4]))
             return t
 
-        d_bytes = sb("d_bytes", G, U8)
-        nc.vector.memset(d_bytes[:].bitcast(I32), 0)
         x_bytes = load_scale_rows("x_bytes", x_scales)
         offs_l = load_list("offs_l", offs)
         k1_l = load_list("k1_l", k1)
-        nc.sync.dma_start(d_bytes[0:P:8, :].bitcast(I32), d_scales[0].bitcast(I32))
-        x_tab = sb("x_tab", T, U32)
-        nc.sync.dma_start(x_tab[:].bitcast(I32), x_words[0].rearrange("p n t -> p (n t)").bitcast(I32))
+        d_bytes = load_scale_rows("d_bytes", d_scales)
+        k2_l = load_list("k2_l", k2)
         d_tab = sb("d_tab", G, U32)
         nc.sync.dma_start(d_tab[:].bitcast(I32), d_words[0].rearrange("p n t -> p (n t)").bitcast(I32))
-        k2_l = load_list("k2_l", k2)
+        x_tab = reuse.tile([P, T], U32, name="x_tab", align_bytes=64, offset=0)
+        nc.sync.dma_start(x_tab[:].bitcast(I32), x_words[0].rearrange("p n t -> p (n t)").bitcast(I32))
         n2_l = load_list("n2_l", n2)
         n1_l = load_list("n1_l", n1)
         n4_l = load_list("n4_l", n4)
@@ -80,7 +79,7 @@ def tile_picked_codewindorder_none_p_kernel(
                 nc.sync.dma_start(plane[a:P:32, :].bitcast(I32), plane[8 * a : P : 32, :].bitcast(I32))
 
         def gather_words(name, lst):
-            got = sb(name + "_got", H, U32)
+            got = keep.tile([P, H], U32, name=name + "_got", tag="words_got", align_bytes=64)
             nc.vector.tensor_copy(got[:], d_tab[:].indirect(lst[:]))
             return got
 
@@ -92,20 +91,23 @@ def tile_picked_codewindorder_none_p_kernel(
             )
             return dealt
 
-        plane1 = sb("plane1", H + S, U8)
         xs_got = sb("xs_got", S, U8)
         nc.vector.tensor_copy(xs_got[:], x_bytes[:].indirect(offs_l[:]))
         w1s_got = sb("w1s_got", H, U8)
         nc.vector.tensor_copy(w1s_got[:], d_bytes[:].indirect(k1_l[:]))
+        w2s_got = sb("w2s_got", H, U8)
+        nc.vector.tensor_copy(w2s_got[:], d_bytes[:].indirect(k2_l[:]))
+        plane1 = keep.tile([P, H + S], U8, name="plane1", tag="d_bytes", align_bytes=64)
         nc.vector.tensor_copy(plane1[:, H:].bitcast(I32), xs_got[:].bitcast(I32))
         nc.vector.tensor_copy(
             plane1[:, :H].rearrange("p (t c i) -> p c t i", t=PACK, i=16),
             w1s_got[:].rearrange("p (c i t) -> p c t i", t=PACK, i=16),
         )
         compact_rows(plane1)
+        w1_got = gather_words("w1w", k1_l)
         xq_w = sb("xq_w", S, U32)
         nc.vector.tensor_copy(xq_w[:], x_tab[:].indirect(offs_l[:]))
-        w1_w = deal_words("w1w", gather_words("w1w", k1_l))
+        w1_w = deal_words("w1w", w1_got)
 
         banks = [psum.tile([P, S], F32, name="bank%d" % b) for b in range(8)]
         for t in range(PACK):
@@ -121,14 +123,19 @@ def tile_picked_codewindorder_none_p_kernel(
             )
             nc.scalar.copy(hw[t][:, :S], banks[t][:])
 
-        w2_s = sb("plane2", H, U8)
-        pick_scales("w2s", k2_l, w2_s[:])
+        w2_got = reuse.tile([P, H], U32, name="w2_got", align_bytes=64, offset=0)
+        nc.vector.tensor_copy(w2_got[:], d_tab[:].indirect(k2_l[:]))
+        w2_s = reuse.tile([P, H], U8, name="plane2", align_bytes=64, offset=4 * H)
+        nc.vector.tensor_copy(
+            w2_s[:].rearrange("p (t c i) -> p c t i", t=PACK, i=16),
+            w2s_got[:].rearrange("p (c i t) -> p c t i", t=PACK, i=16),
+        )
         compact_rows(w2_s)
 
         hg = keep.tile([P, PACK * S], F32, name="hg", tag="hg", align_bytes=64)
         for t in range(PACK):
             nc.scalar.activation(hg[:, t * S : (t + 1) * S], banks[t][:], ACT.Copy, scale=gain[:, t : t + 1])
-        second = [sb("second%d" % t, S, F32) for t in range(PACK)]
+        second = [keep.tile([P, S], F32, name="second%d" % t, tag="second%d" % t, align_bytes=64) for t in range(PACK)]
         diff = sb("diff", PACK * S, F32)
         z_mix = [
             keep.tile([P, PACK * HALF], BF16, name="z_mix%d" % u, tag="z_mix%d" % u, align_bytes=64) for u in range(2)
@@ -156,13 +163,12 @@ def tile_picked_codewindorder_none_p_kernel(
         def quantize(u):
             nc.vector.quantize_mx(out=z_w[u][:].bitcast(FP8X4), scales=z_s[u][:], in_=z_mix[u][:])
 
-        w2_got = gather_words("w2w", k2_l)
+        got4 = w2_got[:].rearrange("p (c i t) -> p c t i", t=PACK, i=4)
+        w2_first = keep.tile([P, P], U32, name="w2_first", tag="second2", align_bytes=64)
+        nc.vector.tensor_copy(w2_first[:].rearrange("p (c i) -> p c i", i=4), got4[:, :, 0, :])
         product(0)
         product(1)
-        got4 = w2_got[:].rearrange("p (c i t) -> p c t i", t=PACK, i=4)
         quantize(0)
-        w2_first = keep.tile([P, P], U32, name="w2_first", tag="hg", align_bytes=64)
-        nc.vector.tensor_copy(w2_first[:].rearrange("p (c i) -> p c i", i=4), got4[:, :, 0, :])
         quantize(1)
         w2_rest = keep.tile([P, 3 * P], U32, name="w2_rest", tag="z_mix0", align_bytes=64)
         nc.vector.tensor_copy(w2_rest[:].rearrange("p (t c i) -> p c t i", t=PACK - 1, i=4), got4[:, :, 1:, :])
@@ -185,7 +191,8 @@ def tile_picked_codewindorder_none_p_kernel(
                 nc.scalar.activation(h2[t][:, u * HALF : (u + 1) * HALF], acc[:, :HALF], ACT.Copy, scale=0.0625)
 
         pb = [sb("pb%d" % t, W, F32) for t in range(PACK)]
-        gap = [sb("gap%d" % t, W, F32) for t in range(PACK)]
+        gaps = keep.tile([P, PACK * W], F32, name="gaps", tag="z_mix0", align_bytes=64)
+        gap = [gaps[:, t * W : (t + 1) * W] for t in range(PACK)]
         up = [sb("up%d" % t, W, F32) for t in range(PACK)]
         drop = [sb("drop%d" % t, W, F32) for t in range(PACK)]
         down = [sb("down%d" % t, W, F32) for t in range(PACK)]
@@ -195,9 +202,12 @@ def tile_picked_codewindorder_none_p_kernel(
             for t in ts:
                 nc.vector.tensor_copy(pb[t][:], h2[t][:].indirect(n4_l[:]))
             for t in ts:
-                nc.vector.tensor_tensor(gap[t][:], h2[t][:].indirect(n3_l[:]), pb[t][:], ALU.subtract)
-                nc.scalar.activation(up[t][:], gap[t][:], ACT.Relu)
-                nc.scalar.activation(drop[t][:], gap[t][:], ACT.Relu, scale=-1.0)
+                nc.vector.tensor_tensor(gap[t], h2[t][:].indirect(n3_l[:]), pb[t][:], ALU.subtract)
+            for t in ts:
+                nc.scalar.activation(up[t][:], gap[t], ACT.Relu)
+            for t in ts:
+                nc.scalar.activation(drop[t][:], gap[t], ACT.Relu, scale=-1.0)
+            for t in ts:
                 nc.scalar.activation(down[t][:], drop[t][:], ACT.Copy, scale=-1.0)
         for ts in ((0, 1), (2, 3)):
             for t in ts:

from contextlib import ExitStack

import concourse.mybir as mybir

K, T, S, G, H, W = 512, 1024, 512, 2048, 512, 256
FLOPS = 2 * K * H * S * 2

F32 = mybir.dt.float32
BF16 = mybir.dt.bfloat16
I32 = mybir.dt.int32
U32 = mybir.dt.uint32
U16 = mybir.dt.uint16
U8 = mybir.dt.uint8
FP8X4 = mybir.dt.float8_e4m3fn_x4
ALU = mybir.AluOpType
ACT = mybir.ActivationFunctionType

P = 128
PACK = 4
HALF = S // 2


def tile_picked_codewindorder_none_p_kernel(
    tc, x_words, x_scales, d_words, d_scales, gs, offs, k1, n1, n2, k2, n3, n4, out
):
    nc = tc.nc
    with ExitStack() as ctx:
        keep = ctx.enter_context(tc.tile_pool(name="keep", bufs=1))
        reuse = ctx.enter_context(tc.tile_pool(name="reuse", bufs=1))
        psum = ctx.enter_context(tc.psum_pool(name="psum", bufs=1))

        def sb(name, cols, dtype):
            return keep.tile([P, cols], dtype, name=name, align_bytes=64)

        def load_list(name, src):
            t = sb(name, src.shape[1], U16)
            nc.sync.dma_start(t[:], src)
            return t

        def load_scale_rows(name, src):
            cols = src.shape[2]
            t = keep.tile([P, cols], U8, name=name, tag=name, align_bytes=64)
            rows = src[0].bitcast(I32)
            nc.sync.dma_start(t[:].bitcast(I32), rows.unsqueeze(1).to_broadcast([16, 8, cols // 4]))
            return t

        x_bytes = load_scale_rows("x_bytes", x_scales)
        offs_l = load_list("offs_l", offs)
        k1_l = load_list("k1_l", k1)
        d_bytes = load_scale_rows("d_bytes", d_scales)
        k2_l = load_list("k2_l", k2)
        d_tab = sb("d_tab", G, U32)
        nc.sync.dma_start(d_tab[:].bitcast(I32), d_words[0].rearrange("p n t -> p (n t)").bitcast(I32))
        x_tab = reuse.tile([P, T], U32, name="x_tab", align_bytes=64, offset=0)
        nc.sync.dma_start(x_tab[:].bitcast(I32), x_words[0].rearrange("p n t -> p (n t)").bitcast(I32))
        n2_l = load_list("n2_l", n2)
        n1_l = load_list("n1_l", n1)
        n4_l = load_list("n4_l", n4)
        n3_l = load_list("n3_l", n3)
        gs_raw = sb("gs_raw", PACK, F32)
        nc.scalar.dma_start(gs_raw[:], gs.rearrange("(p t) o -> p (t o)", t=PACK))
        gain = sb("gain", PACK, F32)
        nc.scalar.activation(gain[:], gs_raw[:], ACT.Copy, scale=0.0625 * 0.0625)

        hw = [sb("hw%d" % t, 2 * S, F32) for t in range(PACK)]
        for t in range(PACK):
            (nc.vector if t < 2 else nc.gpsimd).memset(hw[t][:, S:], 0.0)

        def pick_scales(name, lst, dealt):
            got = sb(name + "_got", H, U8)
            nc.vector.tensor_copy(got[:], d_bytes[:].indirect(lst[:]))
            nc.vector.tensor_copy(
                dealt.rearrange("p (t c i) -> p c t i", t=PACK, i=16),
                got[:].rearrange("p (c i t) -> p c t i", t=PACK, i=16),
            )

        def compact_rows(plane):
            for a in range(1, 4):
                nc.sync.dma_start(plane[a:P:32, :].bitcast(I32), plane[8 * a : P : 32, :].bitcast(I32))

        def gather_words(name, lst):
            got = keep.tile([P, H], U32, name=name + "_got", tag="words_got", align_bytes=64)
            nc.vector.tensor_copy(got[:], d_tab[:].indirect(lst[:]))
            return got

        def deal_words(name, got):
            dealt = sb(name + "_dealt", H, U32)
            nc.vector.tensor_copy(
                dealt[:].rearrange("p (t c i) -> p c t i", t=PACK, i=4),
                got[:].rearrange("p (c i t) -> p c t i", t=PACK, i=4),
            )
            return dealt

        xs_got = sb("xs_got", S, U8)
        nc.vector.tensor_copy(xs_got[:], x_bytes[:].indirect(offs_l[:]))
        w1s_got = sb("w1s_got", H, U8)
        nc.vector.tensor_copy(w1s_got[:], d_bytes[:].indirect(k1_l[:]))
        w2s_got = sb("w2s_got", H, U8)
        nc.vector.tensor_copy(w2s_got[:], d_bytes[:].indirect(k2_l[:]))
        plane1 = keep.tile([P, H + S], U8, name="plane1", tag="d_bytes", align_bytes=64)
        nc.vector.tensor_copy(plane1[:, H:].bitcast(I32), xs_got[:].bitcast(I32))
        nc.vector.tensor_copy(
            plane1[:, :H].rearrange("p (t c i) -> p c t i", t=PACK, i=16),
            w1s_got[:].rearrange("p (c i t) -> p c t i", t=PACK, i=16),
        )
        compact_rows(plane1)
        w1_got = gather_words("w1w", k1_l)
        xq_w = sb("xq_w", S, U32)
        nc.vector.tensor_copy(xq_w[:], x_tab[:].indirect(offs_l[:]))
        w1_w = deal_words("w1w", w1_got)

        banks = [psum.tile([P, S], F32, name="bank%d" % b) for b in range(8)]
        for t in range(PACK):
            cols = slice(t * P, (t + 1) * P)
            nc.tensor.matmul_mx(
                out=banks[t][:],
                lhsT=w1_w[:, cols].bitcast(FP8X4),
                lhsT_scale=plane1[:, cols],
                rhs=xq_w[:].bitcast(FP8X4),
                rhs_scale=plane1[:, H:],
                start=True,
                stop=True,
            )
            nc.scalar.copy(hw[t][:, :S], banks[t][:])

        w2_got = reuse.tile([P, H], U32, name="w2_got", align_bytes=64, offset=0)
        nc.vector.tensor_copy(w2_got[:], d_tab[:].indirect(k2_l[:]))
        w2_s = reuse.tile([P, H], U8, name="plane2", align_bytes=64, offset=4 * H)
        nc.vector.tensor_copy(
            w2_s[:].rearrange("p (t c i) -> p c t i", t=PACK, i=16),
            w2s_got[:].rearrange("p (c i t) -> p c t i", t=PACK, i=16),
        )
        compact_rows(w2_s)

        hg = keep.tile([P, PACK * S], F32, name="hg", tag="hg", align_bytes=64)
        for t in range(PACK):
            nc.scalar.activation(hg[:, t * S : (t + 1) * S], banks[t][:], ACT.Copy, scale=gain[:, t : t + 1])
        second = [keep.tile([P, S], F32, name="second%d" % t, tag="second%d" % t, align_bytes=64) for t in range(PACK)]
        diff = sb("diff", PACK * S, F32)
        z_mix = [
            keep.tile([P, PACK * HALF], BF16, name="z_mix%d" % u, tag="z_mix%d" % u, align_bytes=64) for u in range(2)
        ]
        z_w = [sb("z_w%d" % u, HALF, U32) for u in range(2)]
        z_s = [sb("z_s%d" % u, HALF, U8) for u in range(2)]

        for ts in ((0, 1), (2, 3)):
            for t in ts:
                nc.vector.tensor_copy(second[t][:], hw[t][:].indirect(n2_l[:]))
            for t in ts:
                nc.vector.tensor_tensor(
                    diff[:, t * S : (t + 1) * S], hw[t][:].indirect(n1_l[:]), second[t][:], ALU.subtract
                )

        def product(u):
            pairs = slice(u * HALF // 2, (u + 1) * HALF // 2)
            nc.vector.tensor_tensor(
                z_mix[u][:].rearrange("p (c i t) -> p c t i", t=PACK, i=2),
                diff[:].rearrange("p (t c i) -> p c t i", t=PACK, i=2)[:, pairs],
                hg[:].rearrange("p (t c i) -> p c t i", t=PACK, i=2)[:, pairs],
                ALU.mult,
            )

        def quantize(u):
            nc.vector.quantize_mx(out=z_w[u][:].bitcast(FP8X4), scales=z_s[u][:], in_=z_mix[u][:])

        got4 = w2_got[:].rearrange("p (c i t) -> p c t i", t=PACK, i=4)
        w2_first = keep.tile([P, P], U32, name="w2_first", tag="second2", align_bytes=64)
        nc.vector.tensor_copy(w2_first[:].rearrange("p (c i) -> p c i", i=4), got4[:, :, 0, :])
        product(0)
        product(1)
        quantize(0)
        quantize(1)
        w2_rest = keep.tile([P, 3 * P], U32, name="w2_rest", tag="z_mix0", align_bytes=64)
        nc.vector.tensor_copy(w2_rest[:].rearrange("p (t c i) -> p c t i", t=PACK - 1, i=4), got4[:, :, 1:, :])
        w2_w = [w2_first[:]] + [w2_rest[:, (t - 1) * P : t * P] for t in range(1, PACK)]

        h2 = [sb("h2_%d" % t, S, F32) for t in range(PACK)]
        for t in range(PACK):
            cols = slice(t * P, (t + 1) * P)
            for u in range(2):
                acc = banks[4 * (1 - u) + t]
                nc.tensor.matmul_mx(
                    out=acc[:, :HALF],
                    lhsT=w2_w[t].bitcast(FP8X4),
                    lhsT_scale=w2_s[:, cols],
                    rhs=z_w[u][:].bitcast(FP8X4),
                    rhs_scale=z_s[u][:],
                    start=True,
                    stop=True,
                )
                nc.scalar.activation(h2[t][:, u * HALF : (u + 1) * HALF], acc[:, :HALF], ACT.Copy, scale=0.0625)

        pb = [sb("pb%d" % t, W, F32) for t in range(PACK)]
        gaps = keep.tile([P, PACK * W], F32, name="gaps", tag="z_mix0", align_bytes=64)
        gap = [gaps[:, t * W : (t + 1) * W] for t in range(PACK)]
        up = [sb("up%d" % t, W, F32) for t in range(PACK)]
        drop = [sb("drop%d" % t, W, F32) for t in range(PACK)]
        down = [sb("down%d" % t, W, F32) for t in range(PACK)]
        res = [sb("res%d" % t, S, F32) for t in range(PACK)]
        out_rows = out.rearrange("(p t) n -> t p n", t=PACK)
        for ts in ((0, 1), (2, 3)):
            for t in ts:
                nc.vector.tensor_copy(pb[t][:], h2[t][:].indirect(n4_l[:]))
            for t in ts:
                nc.vector.tensor_tensor(gap[t], h2[t][:].indirect(n3_l[:]), pb[t][:], ALU.subtract)
            for t in ts:
                nc.scalar.activation(up[t][:], gap[t], ACT.Relu)
            for t in ts:
                nc.scalar.activation(drop[t][:], gap[t], ACT.Relu, scale=-1.0)
            for t in ts:
                nc.scalar.activation(down[t][:], drop[t][:], ACT.Copy, scale=-1.0)
        for ts in ((0, 1), (2, 3)):
            for t in ts:
                nc.vector.tensor_tensor(res[t][:].indirect(n3_l[:]), pb[t][:], up[t][:], ALU.add)
            for t in ts:
                nc.vector.tensor_tensor(res[t][:].indirect(n4_l[:]), pb[t][:], down[t][:], ALU.add)
                nc.sync.dma_start(out_rows[t], res[t][:])
